import numpy as np, ml_dtypes
CORES = [0,1,2,3,4,5,6,7]
N = 8
ROOT = 3
def setup_inputs(rng):
    return {"x": rng.standard_normal((N, 128, 512), dtype=np.float32).astype(ml_dtypes.bfloat16)}
def reference(x):
    y = np.full((N, 128, N * 512), np.nan, x.dtype)
    y[ROOT] = np.concatenate(list(x), axis=1)
    return {"y": y}

SCRATCH = {
    "stage": ("sbuf", [128, 512], "bfloat16"),
    "land": ("sbuf", [128, 4096], "bfloat16"),
}
SEMAPHORES = ["loaded", "read", "arrived", "stored"]

BLOCK = 512


def rank_program(g, core, T, topo):
    rank = T.rank_of(core)
    if rank is None:
        return
    n = len(T.cores)
    root_rank = 3
    root = T.cores[root_rank]
    cols = slice(BLOCK * rank, BLOCK * (rank + 1))

    if core != root:
        g.sync.dma_start(T.stage[:], T.x[:]).then_inc(T.sem.loaded, 16)
        g.wait_ge(T.sem.loaded, 16)
        rid, pid, _se = topo.addr(root)
        g.remote_dma(T.land[:, cols], T.stage[:], T.sem.arrived, T.sem.read, pid, rid,
                     topo.mask(core, root))
        g.wait_ge(T.sem.read, 16)
        return

    q = g.sync
    q.dma_start(T.land[:, cols], T.x[:]).then_inc(T.sem.loaded, 16)
    q.wait_ge(T.sem.loaded, 16)
    q.wait_ge(T.sem.arrived, 16 * (n - 1))
    q.dma_start(T.y[:], T.land[:]).then_inc(T.sem.stored, 16)
    q.wait_ge(T.sem.stored, 16)
